import numpy as np
import ml_dtypes


def mxq(x, axis, fmt="e4m3"):
    dtype, down = {"e4m3": (ml_dtypes.float8_e4m3fn, 7), "e5m2": (ml_dtypes.float8_e5m2, 14)}[fmt]
    v = np.moveaxis(np.asarray(x, np.float32).astype(ml_dtypes.bfloat16).astype(np.float64), axis, -1)
    blocks = v.reshape(v.shape[:-1] + (-1, 32))
    amax = np.abs(blocks).max(-1, keepdims=True)
    byte = np.maximum(np.where(amax > 0, np.frexp(amax)[1] - 1 + 127, 0) - down, 1)
    scale = np.exp2(byte - 127.0)
    codes = (blocks / scale).astype(np.float32).astype(dtype).astype(np.float64)
    return np.moveaxis((codes * scale).reshape(v.shape), -1, axis)


WIDE = False


def mx_kscale(k, group=512):
    if not WIDE:
        return np.ones(k)
    levels = np.array([10, -10, 5, -5, 0])
    if group != 512:
        return np.exp2(np.random.permutation(np.resize(levels, k // group))).repeat(group)
    if k % 512:
        return np.exp2(np.random.permutation(np.resize(levels, k // 32))).repeat(32)
    a = np.empty((k // 512, 16))
    for p in range(k // 512):
        a[p, :8] = np.random.permutation(np.resize(levels, 8))
        for g in range(8):
            far = levels[np.abs(levels - a[p, g]) >= 10]
            a[p, g + 8] = far[np.random.randint(len(far))]
    return np.exp2(a.ravel()).repeat(32)


def f64(x):
    return np.asarray(x).astype(np.float64)


E2M1 = np.array([0.0, 0.5, 1.0, 1.5, 2.0, 3.0, 4.0, 6.0, -0.0, -0.5, -1.0, -1.5, -2.0, -3.0, -4.0, -6.0])


def pack_group(w):
    k, n = w.shape
    w = f64(np.asarray(w, np.float32).astype(ml_dtypes.bfloat16)).reshape(k // 32, 32, n)
    amax = np.abs(w).max(1)
    mant, ex = np.frexp(amax / 6.0)
    byte = np.clip(np.where(amax > 0, np.where(mant > 0.5, ex, ex - 1) + 127, 1), 1, 254)
    scaled = (w * np.exp2(127.0 - byte)[:, None, :]).reshape(k, n).astype(np.float32)
    c = np.ascontiguousarray(scaled.reshape(k // 4, 4, n).transpose(0, 2, 1)).astype(ml_dtypes.float4_e2m1fn).view(np.uint8) & 0xF
    return np.ascontiguousarray((c[..., 0::2] | (c[..., 1::2] << 4)).reshape(k // 4, 2 * n)), byte.astype(np.uint8)


def unpack_group(words, scales):
    p, n = words.shape[0], scales.shape[1]
    words = np.ascontiguousarray(words).reshape(p, n, 2)
    nib = np.empty((p, n, 4), np.uint8)
    nib[..., 0::2] = words & 0xF
    nib[..., 1::2] = words >> 4
    return E2M1[nib].transpose(0, 2, 1).reshape(4 * p, n) * np.repeat(np.exp2(scales.astype(np.float64) - 127.0), 32, axis=0)


def silu(v):
    return v / (1.0 + np.exp(-v))


G, D, M, N = 4, 256, 128, 1024


def setup_inputs():
    n = np.random.standard_normal
    s = mx_kscale(D, 0)[:, None]
    w_ = [pack_group(w) for w in n((G, D, M)) / np.sqrt(D) / s]
    u_ = [pack_group(w) for w in n((G, D, M)) / np.sqrt(D) / s]
    return {
        "x": (n((G, D, N)) * s).astype(np.float32),
        "w_words": np.stack([w[0] for w in w_]),
        "w_scales": np.stack([w[1] for w in w_]),
        "u_words": np.stack([w[0] for w in u_]),
        "u_scales": np.stack([w[1] for w in u_]),
        "r": n((G, M, N)).astype(np.float32),
    }


def reference(x, w_words, w_scales, u_words, u_scales, r):
    xq = mxq(f64(x), 1, "e4m3")
    h = np.stack([unpack_group(w_words[g], w_scales[g]) for g in range(G)]).transpose(0, 2, 1) @ xq
    g = np.stack([unpack_group(u_words[g], u_scales[g]) for g in range(G)]).transpose(0, 2, 1) @ xq
    y = silu(h) * g
    y = y + f64(r)
    return y

@@ -1,0 +1,168 @@
+from contextlib import ExitStack
+
+import concourse.mybir as mybir
+
+G, D, M, N = 4, 256, 128, 1024
+FLOPS = 2 * 2 * G * D * M * N
+
+F32 = mybir.dt.float32
+BF16 = mybir.dt.bfloat16
+I32 = mybir.dt.int32
+U32 = mybir.dt.uint32
+U8 = mybir.dt.uint8
+FP8X4 = mybir.dt.float8_e4m3fn_x4
+FP4X4 = mybir.dt.float4_e2m1fn_x4
+SILU = mybir.ActivationFunctionType.Silu
+MULT = mybir.AluOpType.mult
+ADD = mybir.AluOpType.add
+
+P = 128
+PACK = 4
+ROWS = D // PACK
+SIDE = P // ROWS
+PAIRS = G // SIDE
+COLS = 512
+HALVES = N // COLS
+CHUNKS = PAIRS * HALVES
+RUN = 2
+VECTOR_COLS = [512,320,256,256]
+PIECES = [[(0, 256), (256, 512)], [(0, 512)], [(0, 512)], [(0, 512)]]
+
+
+def tile_rows_gglu_silu_res_kernel(tc, x, w_words, w_scales, u_words, u_scales, r, out):
+    nc = tc.nc
+    with ExitStack() as ctx:
+        sb = ctx.enter_context(tc.tile_pool(name="sb", bufs=1))
+        ps = ctx.enter_context(tc.psum_pool(name="ps", bufs=1))
+
+        def per_chunk(name, shape, dtype):
+            return [sb.tile(shape, dtype, name="%s%d" % (name, k), align_bytes=64) for k in range(CHUNKS)]
+
+        raw = [
+            [sb.tile([P, PACK, hi - lo], F32, name="raw%d_%d" % (k, lo), align_bytes=64) for lo, hi in PIECES[k]]
+            for k in range(CHUNKS)
+        ]
+        packed = per_chunk("packed", [P, COLS, PACK], BF16)
+        codes = per_chunk("codes", [P, COLS], U32)
+        x_plane = per_chunk("x_plane", [P, COLS], U8)
+        act = per_chunk("act", [P, SIDE, COLS], F32)
+        res = per_chunk("res", [P, SIDE, COLS], F32)
+        gated = per_chunk("gated", [P, SIDE, COLS], F32)
+        total = per_chunk("total", [P, SIDE, COLS], F32)
+        w_sb = sb.tile([P, PAIRS, 2 * M], U8, align_bytes=64)
+        u_sb = sb.tile([P, PAIRS, 2 * M], U8, align_bytes=64)
+        w_plane = sb.tile([P, PAIRS, M], U8, align_bytes=64)
+        u_plane = sb.tile([P, PAIRS, M], U8, align_bytes=64)
+        z_bank = [[ps.tile([M, COLS], F32, name="z%d_%d" % (b, c)) for c in range(SIDE)] for b in range(2)]
+        v_bank = [[ps.tile([M, COLS], F32, name="v%d_%d" % (b, c)) for c in range(SIDE)] for b in range(2)]
+
+        def load_x(k, j):
+            a, h = divmod(k, HALVES)
+            lo, hi = PIECES[k][j]
+            rows = x[SIDE * a : SIDE * (a + 1)].rearrange("c (p j) n -> (c p) j n", j=PACK)
+            nc.sync.dma_start(out=raw[k][j][:], in_=rows[:, :, h * COLS + lo : h * COLS + hi])
+
+        def load_words(tile_, words):
+            src = words.rearrange("(a c) p b -> (c p) a b", c=SIDE).bitcast(I32)
+            nc.sync.dma_start(out=tile_[:].bitcast(I32), in_=src)
+
+        def load_plane(queue, plane, scales):
+            src = scales.rearrange("(a c) f m -> (c f) a m", c=SIDE).bitcast(I32)
+            for q in range(4):
+                queue.dma_start(out=plane[32 * q : 32 * q + 4].bitcast(I32), in_=src[4 * q : 4 * q + 4])
+
+        def window(t, k):
+            a, h = divmod(k, HALVES)
+            return t[SIDE * a : SIDE * (a + 1), :, h * COLS : (h + 1) * COLS].rearrange("c m n -> m c n")
+
+        def load_r(k):
+            nc.sync.dma_start(out=res[k][:], in_=window(r, k))
+
+        def pack(copy, k, lo, hi):
+            for j, (p_lo, p_hi) in enumerate(PIECES[k]):
+                s, e = max(lo, p_lo), min(hi, p_hi)
+                if s < e:
+                    copy(
+                        out=packed[k][:, s:e, :].rearrange("p (c i) t -> p c t i", i=RUN),
+                        in_=raw[k][j][:, :, s - p_lo : e - p_lo].rearrange("p t (c i) -> p c t i", i=RUN),
+                    )
+
+        def pack_vector(k):
+            pack(nc.vector.tensor_copy, k, 0, VECTOR_COLS[k])
+
+        def pack_scalar(k):
+            pack(nc.scalar.copy, k, VECTOR_COLS[k], COLS)
+
+        def quantize(k, lo=0, hi=COLS):
+            nc.vector.quantize_mx(
+                out=codes[k][:, lo:hi].bitcast(FP8X4),
+                scales=x_plane[k][:, lo:hi],
+                in_=packed[k][:, lo:hi, :].rearrange("p n t -> p (n t)"),
+            )
+
+        def products(k):
+            a = k // HALVES
+            for c in range(SIDE):
+                rows = slice(ROWS * c, ROWS * (c + 1))
+                for words, plane, banks in ((w_sb, w_plane, z_bank), (u_sb, u_plane, v_bank)):
+                    nc.tensor.matmul_mx(
+                        out=banks[k % 2][c][:],
+                        lhsT=words[rows, a, :].bitcast(FP4X4),
+                        lhsT_scale=plane[rows, a, :],
+                        rhs=codes[k][rows, :].bitcast(FP8X4),
+                        rhs_scale=x_plane[k][rows, :],
+                        start=True,
+                        stop=True,
+                    )
+
+        def silu(k, c):
+            nc.scalar.activation(out=act[k][:, c, :], in_=z_bank[k % 2][c][:], func=SILU)
+
+        def gate(k, c):
+            nc.vector.tensor_tensor(out=gated[k][:, c, :], in0=v_bank[k % 2][c][:], in1=act[k][:, c, :], op=MULT)
+
+        def add(k, c):
+            nc.vector.tensor_tensor(out=total[k][:, c, :], in0=gated[k][:, c, :], in1=res[k][:, c, :], op=ADD)
+
+        def store(k, lo=0, hi=SIDE):
+            nc.sync.dma_start(out=window(out, k)[:, lo:hi, :], in_=total[k][:, lo:hi, :])
+
+        with tc.manual_schedule():
+            nc.vector.memset(w_plane[:].bitcast(I32), 0)
+            nc.vector.memset(u_plane[:].bitcast(I32), 0)
+            load_x(0, 0)
+            load_words(w_sb, w_words)
+            load_plane(nc.sync, w_plane, w_scales)
+            load_x(0, 1)
+            load_x(1, 0)
+            load_words(u_sb, u_words)
+            load_plane(nc.sync, u_plane, u_scales)
+            for k in range(CHUNKS):
+                load_r(k)
+                if k + 2 < CHUNKS:
+                    load_x(k + 2, 0)
+
+            for lo, hi in PIECES[0]:
+                pack(nc.vector.tensor_copy, 0, lo, hi)
+                quantize(0, lo, hi)
+            products(0)
+            for k in range(CHUNKS):
+                ahead = k + 1 < CHUNKS
+                silu(k, 0)
+                if ahead:
+                    pack_vector(k + 1)
+                    pack_scalar(k + 1)
+                gate(k, 0)
+                if ahead:
+                    quantize(k + 1)
+                    products(k + 1)
+                silu(k, 1)
+                gate(k, 1)
+                if ahead:
+                    add(k, 0)
+                    add(k, 1)
+                    store(k)
+                else:
+                    for c in range(SIDE):
+                        add(k, c)
+                        store(k, c, c + 1)

@@ -25,8 +25,8 @@ COLS = 512
 HALVES = N // COLS
 CHUNKS = PAIRS * HALVES
 RUN = 2
-VECTOR_COLS = [512,320,256,256]
-PIECES = [[(0, 256), (256, 512)], [(0, 512)], [(0, 512)], [(0, 512)]]
+VECTOR_COLS = [512,512,192,192]
+PIECES = [[(0, 512)], [(0, 512)], [(0, 512)], [(0, 512)]]
 
 
 def tile_rows_gglu_silu_res_kernel(tc, x, w_words, w_scales, u_words, u_scales, r, out):
@@ -133,36 +133,33 @@ def tile_rows_gglu_silu_res_kernel(tc, x, w_words, w_scales, u_words, u_scales, 
             load_x(0, 0)
             load_words(w_sb, w_words)
             load_plane(nc.sync, w_plane, w_scales)
-            load_x(0, 1)
-            load_x(1, 0)
             load_words(u_sb, u_words)
+            load_x(1, 0)
             load_plane(nc.sync, u_plane, u_scales)
             for k in range(CHUNKS):
-                load_r(k)
                 if k + 2 < CHUNKS:
                     load_x(k + 2, 0)
+                load_r(k)
 
-            for lo, hi in PIECES[0]:
-                pack(nc.vector.tensor_copy, 0, lo, hi)
-                quantize(0, lo, hi)
+            pack_vector(0)
+            quantize(0)
             products(0)
             for k in range(CHUNKS):
                 ahead = k + 1 < CHUNKS
-                silu(k, 0)
                 if ahead:
                     pack_vector(k + 1)
                     pack_scalar(k + 1)
-                gate(k, 0)
+                if k > 0:
+                    add(k - 1, 0)
                 if ahead:
                     quantize(k + 1)
                     products(k + 1)
-                silu(k, 1)
-                gate(k, 1)
-                if ahead:
-                    add(k, 0)
-                    add(k, 1)
-                    store(k)
-                else:
-                    for c in range(SIDE):
-                        add(k, c)
-                        store(k, c, c + 1)
+                if k > 0:
+                    add(k - 1, 1)
+                    store(k - 1)
+                for c in range(SIDE):
+                    silu(k, c)
+                    gate(k, c)
+            for c in range(SIDE):
+                add(CHUNKS - 1, c)
+                store(CHUNKS - 1, c, c + 1)

@@ -24,7 +24,7 @@ PAIRS = G // SIDE
 COLS = 512
 HALVES = N // COLS
 CHUNKS = PAIRS * HALVES
-RUN = 2
+RUN = 4
 VECTOR_COLS = [512,512,192,192]
 PIECES = [[(0, 512)], [(0, 512)], [(0, 512)], [(0, 512)]]
 
@@ -121,8 +121,8 @@ def tile_rows_gglu_silu_res_kernel(tc, x, w_words, w_scales, u_words, u_scales, 
         def gate(k, c):
             nc.vector.tensor_tensor(out=gated[k][:, c, :], in0=v_bank[k % 2][c][:], in1=act[k][:, c, :], op=MULT)
 
-        def add(k, c):
-            nc.vector.tensor_tensor(out=total[k][:, c, :], in0=gated[k][:, c, :], in1=res[k][:, c, :], op=ADD)
+        def add(k, c, engine=nc.vector):
+            engine.tensor_tensor(out=total[k][:, c, :], in0=gated[k][:, c, :], in1=res[k][:, c, :], op=ADD)
 
         def store(k, lo=0, hi=SIDE):
             nc.sync.dma_start(out=window(out, k)[:, lo:hi, :], in_=total[k][:, lo:hi, :])
@@ -154,9 +154,13 @@ def tile_rows_gglu_silu_res_kernel(tc, x, w_words, w_scales, u_words, u_scales, 
                 if ahead:
                     quantize(k + 1)
                     products(k + 1)
-                if k > 0:
+                if k > 0 and ahead:
                     add(k - 1, 1)
                     store(k - 1)
+                if not ahead:
+                    store(k - 1, 0, 1)
+                    add(k - 1, 1, nc.gpsimd)
+                    store(k - 1, 1, 2)
                 for c in range(SIDE):
                     silu(k, c)
                     gate(k, c)

@@ -24,9 +24,11 @@ PAIRS = G // SIDE
 COLS = 512
 HALVES = N // COLS
 CHUNKS = PAIRS * HALVES
+QUADRANT = 32
+LIVE = 4
+BANK_SETS = 2
 RUN = 4
-VECTOR_COLS = [512,512,192,192]
-PIECES = [[(0, 512)], [(0, 512)], [(0, 512)], [(0, 512)]]
+VECTOR_COLS = (512, 512, 256, 256)
 
 
 def tile_rows_gglu_silu_res_kernel(tc, x, w_words, w_scales, u_words, u_scales, r, out):
@@ -38,10 +40,7 @@ def tile_rows_gglu_silu_res_kernel(tc, x, w_words, w_scales, u_words, u_scales, 
         def per_chunk(name, shape, dtype):
             return [sb.tile(shape, dtype, name="%s%d" % (name, k), align_bytes=64) for k in range(CHUNKS)]
 
-        raw = [
-            [sb.tile([P, PACK, hi - lo], F32, name="raw%d_%d" % (k, lo), align_bytes=64) for lo, hi in PIECES[k]]
-            for k in range(CHUNKS)
-        ]
+        raw = per_chunk("raw", [P, PACK, COLS], F32)
         packed = per_chunk("packed", [P, COLS, PACK], BF16)
         codes = per_chunk("codes", [P, COLS], U32)
         x_plane = per_chunk("x_plane", [P, COLS], U8)
@@ -53,60 +52,62 @@ def tile_rows_gglu_silu_res_kernel(tc, x, w_words, w_scales, u_words, u_scales, 
         u_sb = sb.tile([P, PAIRS, 2 * M], U8, align_bytes=64)
         w_plane = sb.tile([P, PAIRS, M], U8, align_bytes=64)
         u_plane = sb.tile([P, PAIRS, M], U8, align_bytes=64)
-        z_bank = [[ps.tile([M, COLS], F32, name="z%d_%d" % (b, c)) for c in range(SIDE)] for b in range(2)]
-        v_bank = [[ps.tile([M, COLS], F32, name="v%d_%d" % (b, c)) for c in range(SIDE)] for b in range(2)]
 
-        def load_x(k, j):
+        def banks(name):
+            return [
+                [ps.tile([M, COLS], F32, name="%s%d_%d" % (name, b, c)) for c in range(SIDE)] for b in range(BANK_SETS)
+            ]
+
+        z_bank = banks("z")
+        v_bank = banks("v")
+
+        def place(k):
             a, h = divmod(k, HALVES)
-            lo, hi = PIECES[k][j]
-            rows = x[SIDE * a : SIDE * (a + 1)].rearrange("c (p j) n -> (c p) j n", j=PACK)
-            nc.sync.dma_start(out=raw[k][j][:], in_=rows[:, :, h * COLS + lo : h * COLS + hi])
+            return slice(SIDE * a, SIDE * (a + 1)), slice(COLS * h, COLS * (h + 1))
 
-        def load_words(tile_, words):
+        def load_x(k):
+            groups, cols = place(k)
+            rows = x[groups].rearrange("c (p t) n -> (c p) t n", t=PACK)
+            nc.sync.dma_start(out=raw[k][:], in_=rows[:, :, cols])
+
+        def load_words(dst, words):
             src = words.rearrange("(a c) p b -> (c p) a b", c=SIDE).bitcast(I32)
-            nc.sync.dma_start(out=tile_[:].bitcast(I32), in_=src)
+            nc.sync.dma_start(out=dst[:].bitcast(I32), in_=src)
 
-        def load_plane(queue, plane, scales):
+        def load_plane(plane, scales):
             src = scales.rearrange("(a c) f m -> (c f) a m", c=SIDE).bitcast(I32)
-            for q in range(4):
-                queue.dma_start(out=plane[32 * q : 32 * q + 4].bitcast(I32), in_=src[4 * q : 4 * q + 4])
+            for q in range(P // QUADRANT):
+                live = plane[QUADRANT * q : QUADRANT * q + LIVE]
+                nc.sync.dma_start(out=live.bitcast(I32), in_=src[LIVE * q : LIVE * (q + 1)])
 
         def window(t, k):
-            a, h = divmod(k, HALVES)
-            return t[SIDE * a : SIDE * (a + 1), :, h * COLS : (h + 1) * COLS].rearrange("c m n -> m c n")
+            groups, cols = place(k)
+            return t[groups, :, cols].rearrange("c m n -> m c n")
 
         def load_r(k):
             nc.sync.dma_start(out=res[k][:], in_=window(r, k))
 
-        def pack(copy, k, lo, hi):
-            for j, (p_lo, p_hi) in enumerate(PIECES[k]):
-                s, e = max(lo, p_lo), min(hi, p_hi)
-                if s < e:
+        def pack(k):
+            split = VECTOR_COLS[k]
+            for copy, lo, hi in ((nc.vector.tensor_copy, 0, split), (nc.scalar.copy, split, COLS)):
+                if lo < hi:
                     copy(
-                        out=packed[k][:, s:e, :].rearrange("p (c i) t -> p c t i", i=RUN),
-                        in_=raw[k][j][:, :, s - p_lo : e - p_lo].rearrange("p t (c i) -> p c t i", i=RUN),
+                        out=packed[k][:, lo:hi, :].rearrange("p (n i) t -> p n t i", i=RUN),
+                        in_=raw[k][:, :, lo:hi].rearrange("p t (n i) -> p n t i", i=RUN),
                     )
 
-        def pack_vector(k):
-            pack(nc.vector.tensor_copy, k, 0, VECTOR_COLS[k])
-
-        def pack_scalar(k):
-            pack(nc.scalar.copy, k, VECTOR_COLS[k], COLS)
-
-        def quantize(k, lo=0, hi=COLS):
+        def multiply(k):
             nc.vector.quantize_mx(
-                out=codes[k][:, lo:hi].bitcast(FP8X4),
-                scales=x_plane[k][:, lo:hi],
-                in_=packed[k][:, lo:hi, :].rearrange("p n t -> p (n t)"),
+                out=codes[k][:].bitcast(FP8X4),
+                scales=x_plane[k][:],
+                in_=packed[k][:].rearrange("p n t -> p (n t)"),
             )
-
-        def products(k):
             a = k // HALVES
             for c in range(SIDE):
                 rows = slice(ROWS * c, ROWS * (c + 1))
-                for words, plane, banks in ((w_sb, w_plane, z_bank), (u_sb, u_plane, v_bank)):
+                for words, plane, bank in ((w_sb, w_plane, z_bank), (u_sb, u_plane, v_bank)):
                     nc.tensor.matmul_mx(
-                        out=banks[k % 2][c][:],
+                        out=bank[k % BANK_SETS][c][:],
                         lhsT=words[rows, a, :].bitcast(FP4X4),
                         lhsT_scale=plane[rows, a, :],
                         rhs=codes[k][rows, :].bitcast(FP8X4),
@@ -115,55 +116,41 @@ def tile_rows_gglu_silu_res_kernel(tc, x, w_words, w_scales, u_words, u_scales, 
                         stop=True,
                     )
 
-        def silu(k, c):
-            nc.scalar.activation(out=act[k][:, c, :], in_=z_bank[k % 2][c][:], func=SILU)
-
         def gate(k, c):
-            nc.vector.tensor_tensor(out=gated[k][:, c, :], in0=v_bank[k % 2][c][:], in1=act[k][:, c, :], op=MULT)
+            b = k % BANK_SETS
+            nc.scalar.activation(out=act[k][:, c, :], in_=z_bank[b][c][:], func=SILU)
+            nc.vector.tensor_tensor(out=gated[k][:, c, :], in0=v_bank[b][c][:], in1=act[k][:, c, :], op=MULT)
 
-        def add(k, c, engine=nc.vector):
+        def finish(engine, k, c):
             engine.tensor_tensor(out=total[k][:, c, :], in0=gated[k][:, c, :], in1=res[k][:, c, :], op=ADD)
-
-        def store(k, lo=0, hi=SIDE):
-            nc.sync.dma_start(out=window(out, k)[:, lo:hi, :], in_=total[k][:, lo:hi, :])
+            nc.sync.dma_start(out=window(out, k)[:, c : c + 1, :], in_=total[k][:, c : c + 1, :])
 
         with tc.manual_schedule():
             nc.vector.memset(w_plane[:].bitcast(I32), 0)
             nc.vector.memset(u_plane[:].bitcast(I32), 0)
-            load_x(0, 0)
+
+            load_x(0)
             load_words(w_sb, w_words)
-            load_plane(nc.sync, w_plane, w_scales)
+            load_plane(w_plane, w_scales)
             load_words(u_sb, u_words)
-            load_x(1, 0)
-            load_plane(nc.sync, u_plane, u_scales)
+            load_x(1)
+            load_plane(u_plane, u_scales)
             for k in range(CHUNKS):
                 if k + 2 < CHUNKS:
-                    load_x(k + 2, 0)
+                    load_x(k + 2)
                 load_r(k)
 
-            pack_vector(0)
-            quantize(0)
-            products(0)
+            pack(0)
+            multiply(0)
             for k in range(CHUNKS):
-                ahead = k + 1 < CHUNKS
-                if ahead:
-                    pack_vector(k + 1)
-                    pack_scalar(k + 1)
+                if k + 1 < CHUNKS:
+                    pack(k + 1)
                 if k > 0:
-                    add(k - 1, 0)
-                if ahead:
-                    quantize(k + 1)
-                    products(k + 1)
-                if k > 0 and ahead:
-                    add(k - 1, 1)
-                    store(k - 1)
-                if not ahead:
-                    store(k - 1, 0, 1)
-                    add(k - 1, 1, nc.gpsimd)
-                    store(k - 1, 1, 2)
+                    finish(nc.vector, k - 1, 0)
+                    finish(nc.gpsimd, k - 1, 1)
+                if k + 1 < CHUNKS:
+                    multiply(k + 1)
                 for c in range(SIDE):
-                    silu(k, c)
                     gate(k, c)
             for c in range(SIDE):
-                add(CHUNKS - 1, c)
-                store(CHUNKS - 1, c, c + 1)
+                finish(nc.vector, CHUNKS - 1, c)

from contextlib import ExitStack

import concourse.mybir as mybir

G, D, M, N = 4, 256, 128, 1024
FLOPS = 2 * 2 * G * D * M * N

F32 = mybir.dt.float32
BF16 = mybir.dt.bfloat16
I32 = mybir.dt.int32
U32 = mybir.dt.uint32
U8 = mybir.dt.uint8
FP8X4 = mybir.dt.float8_e4m3fn_x4
FP4X4 = mybir.dt.float4_e2m1fn_x4
SILU = mybir.ActivationFunctionType.Silu
MULT = mybir.AluOpType.mult
ADD = mybir.AluOpType.add

P = 128
PACK = 4
ROWS = D // PACK
SIDE = P // ROWS
PAIRS = G // SIDE
COLS = 512
HALVES = N // COLS
CHUNKS = PAIRS * HALVES
QUADRANT = 32
LIVE = 4
BANK_SETS = 2
RUN = 4
VECTOR_COLS = (512, 512, 256, 256)


def tile_rows_gglu_silu_res_kernel(tc, x, w_words, w_scales, u_words, u_scales, r, out):
    nc = tc.nc
    with ExitStack() as ctx:
        sb = ctx.enter_context(tc.tile_pool(name="sb", bufs=1))
        ps = ctx.enter_context(tc.psum_pool(name="ps", bufs=1))

        def per_chunk(name, shape, dtype):
            return [sb.tile(shape, dtype, name="%s%d" % (name, k), align_bytes=64) for k in range(CHUNKS)]

        raw = per_chunk("raw", [P, PACK, COLS], F32)
        packed = per_chunk("packed", [P, COLS, PACK], BF16)
        codes = per_chunk("codes", [P, COLS], U32)
        x_plane = per_chunk("x_plane", [P, COLS], U8)
        act = per_chunk("act", [P, SIDE, COLS], F32)
        res = per_chunk("res", [P, SIDE, COLS], F32)
        gated = per_chunk("gated", [P, SIDE, COLS], F32)
        total = per_chunk("total", [P, SIDE, COLS], F32)
        w_sb = sb.tile([P, PAIRS, 2 * M], U8, align_bytes=64)
        u_sb = sb.tile([P, PAIRS, 2 * M], U8, align_bytes=64)
        w_plane = sb.tile([P, PAIRS, M], U8, align_bytes=64)
        u_plane = sb.tile([P, PAIRS, M], U8, align_bytes=64)

        def banks(name):
            return [
                [ps.tile([M, COLS], F32, name="%s%d_%d" % (name, b, c)) for c in range(SIDE)] for b in range(BANK_SETS)
            ]

        z_bank = banks("z")
        v_bank = banks("v")

        def place(k):
            a, h = divmod(k, HALVES)
            return slice(SIDE * a, SIDE * (a + 1)), slice(COLS * h, COLS * (h + 1))

        def load_x(k):
            groups, cols = place(k)
            rows = x[groups].rearrange("c (p t) n -> (c p) t n", t=PACK)
            nc.sync.dma_start(out=raw[k][:], in_=rows[:, :, cols])

        def load_words(dst, words):
            src = words.rearrange("(a c) p b -> (c p) a b", c=SIDE).bitcast(I32)
            nc.sync.dma_start(out=dst[:].bitcast(I32), in_=src)

        def load_plane(plane, scales):
            src = scales.rearrange("(a c) f m -> (c f) a m", c=SIDE).bitcast(I32)
            for q in range(P // QUADRANT):
                live = plane[QUADRANT * q : QUADRANT * q + LIVE]
                nc.sync.dma_start(out=live.bitcast(I32), in_=src[LIVE * q : LIVE * (q + 1)])

        def window(t, k):
            groups, cols = place(k)
            return t[groups, :, cols].rearrange("c m n -> m c n")

        def load_r(k):
            nc.sync.dma_start(out=res[k][:], in_=window(r, k))

        def pack(k):
            split = VECTOR_COLS[k]
            for copy, lo, hi in ((nc.vector.tensor_copy, 0, split), (nc.scalar.copy, split, COLS)):
                if lo < hi:
                    copy(
                        out=packed[k][:, lo:hi, :].rearrange("p (n i) t -> p n t i", i=RUN),
                        in_=raw[k][:, :, lo:hi].rearrange("p t (n i) -> p n t i", i=RUN),
                    )

        def multiply(k):
            nc.vector.quantize_mx(
                out=codes[k][:].bitcast(FP8X4),
                scales=x_plane[k][:],
                in_=packed[k][:].rearrange("p n t -> p (n t)"),
            )
            a = k // HALVES
            for c in range(SIDE):
                rows = slice(ROWS * c, ROWS * (c + 1))
                for words, plane, bank in ((w_sb, w_plane, z_bank), (u_sb, u_plane, v_bank)):
                    nc.tensor.matmul_mx(
                        out=bank[k % BANK_SETS][c][:],
                        lhsT=words[rows, a, :].bitcast(FP4X4),
                        lhsT_scale=plane[rows, a, :],
                        rhs=codes[k][rows, :].bitcast(FP8X4),
                        rhs_scale=x_plane[k][rows, :],
                        start=True,
                        stop=True,
                    )

        def gate(k, c):
            b = k % BANK_SETS
            nc.scalar.activation(out=act[k][:, c, :], in_=z_bank[b][c][:], func=SILU)
            nc.vector.tensor_tensor(out=gated[k][:, c, :], in0=v_bank[b][c][:], in1=act[k][:, c, :], op=MULT)

        def finish(engine, k, c):
            engine.tensor_tensor(out=total[k][:, c, :], in0=gated[k][:, c, :], in1=res[k][:, c, :], op=ADD)
            nc.sync.dma_start(out=window(out, k)[:, c : c + 1, :], in_=total[k][:, c : c + 1, :])

        with tc.manual_schedule():
            nc.vector.memset(w_plane[:].bitcast(I32), 0)
            nc.vector.memset(u_plane[:].bitcast(I32), 0)

            load_x(0)
            load_words(w_sb, w_words)
            load_plane(w_plane, w_scales)
            load_words(u_sb, u_words)
            load_x(1)
            load_plane(u_plane, u_scales)
            for k in range(CHUNKS):
                if k + 2 < CHUNKS:
                    load_x(k + 2)
                load_r(k)

            pack(0)
            multiply(0)
            for k in range(CHUNKS):
                if k + 1 < CHUNKS:
                    pack(k + 1)
                if k > 0:
                    finish(nc.vector, k - 1, 0)
                    finish(nc.gpsimd, k - 1, 1)
                if k + 1 < CHUNKS:
                    multiply(k + 1)
                for c in range(SIDE):
                    gate(k, c)
            for c in range(SIDE):
                finish(nc.vector, CHUNKS - 1, c)
